import numpy as np
import ml_dtypes


def mxq(x, axis, fmt="e4m3"):
    dtype, down = {"e4m3": (ml_dtypes.float8_e4m3fn, 7), "e5m2": (ml_dtypes.float8_e5m2, 14)}[fmt]
    v = np.moveaxis(np.asarray(x, np.float32).astype(ml_dtypes.bfloat16).astype(np.float64), axis, -1)
    blocks = v.reshape(v.shape[:-1] + (-1, 32))
    amax = np.abs(blocks).max(-1, keepdims=True)
    byte = np.maximum(np.where(amax > 0, np.frexp(amax)[1] - 1 + 127, 0) - down, 1)
    scale = np.exp2(byte - 127.0)
    codes = (blocks / scale).astype(np.float32).astype(dtype).astype(np.float64)
    return np.moveaxis((codes * scale).reshape(v.shape), -1, axis)


WIDE = False


def mx_kscale(k):
    if not WIDE:
        return np.ones(k)
    levels = np.array([30, -30])
    if k % 512:
        return np.exp2(np.random.permutation(np.resize(levels, k // 32))).repeat(32)
    a = np.empty((k // 512, 16))
    for p in range(k // 512):
        a[p, :8] = np.random.permutation(np.resize(levels, 8))
        for g in range(8):
            far = levels[np.abs(levels - a[p, g]) >= 10]
            a[p, g + 8] = far[np.random.randint(len(far))]
    return np.exp2(a.ravel()).repeat(32)


def f64(x):
    return np.asarray(x).astype(np.float64)


def striped(idx):
    return np.tile(idx.reshape(-1, 16).T, (8, 1)).astype(np.uint16)


def unstriped(offs):
    return offs[:16].T.reshape(-1).astype(np.int64)


def d_silu(v):
    s = 1.0 / (1.0 + np.exp(-np.maximum(v, -700.0)))
    return s * (1.0 + v * (1.0 - s))


K, T, E, C, H, N = 128, 1536, 2, 512, 1024, 512


def by_expert(wq, xq):
    return np.concatenate([wq[e].T @ xq[:, e * C:(e + 1) * C] for e in range(E)], axis=1)


def setup_inputs():
    n = np.random.standard_normal
    s = mx_kscale(N)[:, None]
    u = mx_kscale(H)
    return {
        "dyT": (n((N, T)) * s).astype(np.float32),
        "a": n((H, E * C)).astype(np.float32),
        "w2": (n((E, N, H)) / np.sqrt(N) / s[None] * u[None, None, :]).astype(np.float32),
        "w1": (n((E, H, K)) / np.sqrt(H) / u[None, :, None]).astype(np.float32),
        "gate": np.tile(np.random.uniform(0.2, 1.0, E * C), (N, 1)).astype(np.float32),
        "offs": striped(np.random.permutation(T)[:E * C]),
    }


def reference(dyT, a, w2, w1, gate, offs):
    idx = unstriped(offs)
    gq = mxq(f64(gate) * f64(dyT)[:, idx], 0, "e5m2")
    dh = by_expert(mxq(f64(w2), 1, "e4m3"), gq)
    da = dh * d_silu(f64(a))
    dx = by_expert(mxq(f64(w1), 1, "e4m3"), mxq(da, 0, "e5m2"))
    out = np.zeros((K, T))
    out[:, idx] = dx
    return out

@@ -1,0 +1,358 @@
+from contextlib import ExitStack
+
+import concourse.mybir as mybir
+
+F32 = mybir.dt.float32
+BF16 = mybir.dt.bfloat16
+U32 = mybir.dt.uint32
+U16 = mybir.dt.uint16
+U8 = mybir.dt.uint8
+E4M3 = mybir.dt.float8_e4m3fn_x4
+E5M2 = mybir.dt.float8_e5m2_x4
+ADD = mybir.AluOpType.add
+MULT = mybir.AluOpType.mult
+COPY = mybir.ActivationFunctionType.Copy
+SIGMOID = mybir.ActivationFunctionType.Sigmoid
+SILU = mybir.ActivationFunctionType.Silu
+
+P = 128
+K, T, E, C, H, N = 128, 1536, 2, 512, 1024, 512
+S = E * C
+PACK = 4
+HALVES = H // 512
+
+FLOPS = 2 * S * N * H + 2 * S * H * K
+BYTES = 4 * (N * T + H * S + E * N * H + E * H * K + S + K * T) + 2 * S
+
+
+def tile_moe_bdx_mlp_silu_kernel(tc, dyT, a, w2, w1, gate, offs, out):
+    nc = tc.nc
+    dy_rows = dyT.rearrange("(p t) s -> p t s", t=PACK)
+    a_rows = a.rearrange("(h p t) s -> p h t s", h=HALVES, t=PACK)
+    w2_rows = w2.rearrange("e (p j) i -> p e j i", j=PACK)
+    w1_rows = w1.rearrange("e (h p j) k -> p (e h) j k", h=HALVES, j=PACK)
+
+    with ExitStack() as ctx:
+        lists = ctx.enter_context(tc.tile_pool(name="lists", bufs=1))
+        keep = ctx.enter_context(tc.tile_pool(name="keep", bufs=1))
+        ring = ctx.enter_context(tc.tile_pool(name="ring", bufs=2))
+        banks = ctx.enter_context(tc.psum_pool(name="banks", bufs=6))
+        sums = ctx.enter_context(tc.psum_pool(name="sums", bufs=2))
+
+        offsets = lists.tile([P, S // 16], U16, name="offsets")
+        gates = keep.tile([P, S], F32, name="gates")
+        dy = [keep.tile([P, T], F32, name=f"dy{t}") for t in range(PACK)]
+        pre = {}
+        aux = {}
+        w2_raw = {}
+        for e in range(E):
+            for h in range(HALVES):
+                pre[e, h] = keep.tile([P, PACK, C], F32, name=f"pre{e}{h}")
+                aux[e, h] = keep.tile([P, PACK, C], F32, name=f"aux{e}{h}")
+                w2_raw[e, h] = keep.tile([P, PACK, 512], F32, name=f"w2raw{e}{h}")
+        w1_raw = keep.tile([P, E * HALVES, PACK, K], F32, name="w1raw")
+        result = keep.tile([P, T], F32, name="result")
+        one = keep.tile([P, 1], F32, name="one")
+
+        def load_offs():
+            nc.sync.dma_start(offsets[:], offs)
+
+        def load_gate(e):
+            nc.sync.dma_start(gates[:, e * C : (e + 1) * C], gate[0:P, e * C : (e + 1) * C])
+
+        def load_dy(t):
+            nc.sync.dma_start(dy[t][:], dy_rows[:, t, :])
+
+        def load_a(e, h, t0=0, t1=4):
+            nc.sync.dma_start(pre[e, h][:, t0:t1, :], a_rows[:, h, t0:t1, e * C : (e + 1) * C])
+
+        def load_w2(e, h):
+            nc.sync.dma_start(w2_raw[e, h][:], w2_rows[:, e, :, h * 512 : (h + 1) * 512])
+
+        def load_w1():
+            nc.sync.dma_start(w1_raw[:], w1_rows)
+
+        first_of = {}
+
+        def sigmoid(e, h, t0=0, t1=4, bias=0.0):
+            first = first_of.setdefault((e, h), "sig") == "sig"
+            dst = aux[e, h] if first else pre[e, h]
+            nc.scalar.activation(dst[:, t0:t1, :], pre[e, h][:, t0:t1, :], SIGMOID, scale=-1.0, bias=bias)
+
+        def silu(e, h, t0=0, t1=4, bias=0.0):
+            first = first_of.setdefault((e, h), "silu") == "silu"
+            dst = aux[e, h] if first else pre[e, h]
+            nc.scalar.activation(dst[:, t0:t1, :], pre[e, h][:, t0:t1, :], SILU, bias=bias)
+
+        def token(e, h, func, name):
+            z = keep.tile([P, 1], F32, name=name)
+            src = aux[e, h] if first_of[e, h] == func else pre[e, h]
+            nc.scalar.activation(z[:], src[:, PACK - 1, C - 1 : C], COPY, scale=0.0)
+            return z[:]
+
+        def weigh(e, h):
+            y, s = (pre[e, h], aux[e, h]) if first_of[e, h] == "sig" else (aux[e, h], pre[e, h])
+            nc.vector.scalar_tensor_tensor(aux[e, h][:], y[:], -1.0, s[:], ADD, MULT)
+
+        g_rows = keep.tile([P, PACK, S], F32, name="grows")
+
+        def gather(t, e):
+            cols = slice(e * C, (e + 1) * C)
+            nc.vector.tensor_tensor(
+                g_rows[:, t, cols], dy[t][:].indirect(offsets[:, e * (C // 16) : (e + 1) * (C // 16)]), gates[:, cols], MULT
+            )
+
+        def copy_on(engine, dst, src):
+            if engine == "S":
+                nc.scalar.copy(dst, src)
+            elif engine == "V":
+                nc.vector.tensor_copy(dst, src)
+            else:
+                nc.gpsimd.tensor_scalar(dst, src, 1.0, 0.0, MULT, ADD)
+
+        g_pairs = {}
+        g_codes = {}
+        g_scales = {}
+
+        def lay_g(e, engine):
+            g_pairs[e] = ring.tile([P, C, PACK], BF16, name="gpairs", align_bytes=64)
+            copy_on(
+                engine,
+                g_pairs[e][:].rearrange("p (c i) t -> p c t i", i=4),
+                g_rows[:, :, e * C : (e + 1) * C].rearrange("p t (c i) -> p c t i", i=4),
+            )
+
+        def quant_g(e):
+            g_codes[e] = keep.tile([P, C], U32, name=f"gcodes{e}", align_bytes=64)
+            g_scales[e] = keep.tile([P, C], U8, name=f"gscales{e}", align_bytes=64)
+            nc.vector.quantize_mx(out=g_codes[e][:].bitcast(E5M2), scales=g_scales[e][:], in_=g_pairs[e][:].rearrange("p c t -> p (c t)"))
+
+        w2_pairs = {}
+        w2_codes = {}
+        w2_scales = {}
+
+        def lay_w2(e, h, engine, part=None):
+            if (e, h) not in w2_pairs:
+                w2_pairs[e, h] = ring.tile([P, 4, 128, 4], BF16, name="w2pairs", align_bytes=64)
+            m = slice(0, 128) if part is None else slice(part * 64, part * 64 + 64)
+            src = w2_raw[e, h][:] if part is None else w2_raw[e, h][:, :, part * 256 : part * 256 + 256]
+            copy_on(
+                engine,
+                w2_pairs[e, h][:, :, m, :].rearrange("p t m j -> p m j t"),
+                src.rearrange("p j (m t) -> p m j t", t=4),
+            )
+
+        def quant_w2(e, h):
+            w2_codes[e, h] = keep.tile([P, 512], U32, name=f"w2codes{e}{h}", align_bytes=64)
+            w2_scales[e, h] = keep.tile([P, 512], U8, name=f"w2scales{e}{h}", align_bytes=64)
+            nc.vector.quantize_mx(
+                out=w2_codes[e, h][:].bitcast(E4M3), scales=w2_scales[e, h][:], in_=w2_pairs[e, h][:].rearrange("p t m j -> p (t m j)")
+            )
+
+        w1_pairs = keep.tile([P, E * HALVES, K, PACK], BF16, name="w1pairs", align_bytes=64)
+        w1_codes = keep.tile([P, E * HALVES * K], U32, name="w1codes", align_bytes=64)
+        w1_scales = keep.tile([P, E * HALVES * K], U8, name="w1scales", align_bytes=64)
+
+        def lay_w1(engine):
+            for u in range(E * HALVES):
+                copy_on(
+                    engine,
+                    w1_pairs[:, u].rearrange("p (c i) j -> p c j i", i=4),
+                    w1_raw[:, u].rearrange("p j (c i) -> p c j i", i=4),
+                )
+
+        def quant_w1():
+            nc.vector.quantize_mx(out=w1_codes[:].bitcast(E4M3), scales=w1_scales[:], in_=w1_pairs[:].rearrange("p u k j -> p (u k j)"))
+
+        bank = {}
+
+        def product(e, h, t):
+            bank[e, h, t] = banks.tile([P, C], F32, name="bank")
+            cols = slice(t * P, (t + 1) * P)
+            nc.tensor.matmul_mx(
+                out=bank[e, h, t][:],
+                lhsT=w2_codes[e, h][:, cols].bitcast(E4M3),
+                lhsT_scale=w2_scales[e, h][:, cols],
+                rhs=g_codes[e][:].bitcast(E5M2),
+                rhs_scale=g_scales[e][:],
+                start=True,
+                stop=True,
+            )
+
+        dh = {}
+        da_pairs = {}
+        da_planes = {}
+        da_codes = {}
+        da_scales = {}
+
+        def evac(e, h, t):
+            if (e, h) not in dh:
+                dh[e, h] = ring.tile([P, PACK, C], F32, name="dh")
+            nc.scalar.copy(dh[e, h][:, t, :], bank[e, h, t][:])
+
+        def deriv(e, h):
+            da_pairs[e, h] = ring.tile([P, C, PACK], BF16, name="dapairs", align_bytes=64)
+            nc.vector.scalar_tensor_tensor(
+                da_pairs[e, h][:],
+                aux[e, h][:].rearrange("p t c -> p c t"),
+                1.0,
+                dh[e, h][:].rearrange("p t c -> p c t"),
+                ADD,
+                MULT,
+            )
+
+        def deriv_bank(e, h, t):
+            if (e, h) not in da_planes:
+                da_planes[e, h] = ring.tile([P, PACK, C], BF16, name="daplanes")
+            nc.vector.scalar_tensor_tensor(da_planes[e, h][:, t, :], aux[e, h][:, t, :], 1.0, bank[e, h, t][:], ADD, MULT)
+
+        def lay_da(e, h, engine):
+            da_pairs[e, h] = ring.tile([P, C, PACK], BF16, name="dapairs", align_bytes=64)
+            copy_on(
+                engine,
+                da_pairs[e, h][:].rearrange("p (c i) t -> p c t i", i=4),
+                da_planes[e, h][:].rearrange("p t (c i) -> p c t i", i=4),
+            )
+
+        def quant_da(e, h):
+            da_codes[e, h] = ring.tile([P, C], U32, name="dacodes", align_bytes=64)
+            da_scales[e, h] = ring.tile([P, C], U8, name="dascales", align_bytes=64)
+            nc.vector.quantize_mx(
+                out=da_codes[e, h][:].bitcast(E5M2), scales=da_scales[e, h][:], in_=da_pairs[e, h][:].rearrange("p c t -> p (c t)")
+            )
+
+        dx = {}
+
+        def second(e, h):
+            if h == 0:
+                dx[e] = sums.tile([P, C], F32, name="dx")
+            u = e * HALVES + h
+            cols = slice(u * K, (u + 1) * K)
+            nc.tensor.matmul_mx(
+                out=dx[e][:],
+                lhsT=w1_codes[:, cols].bitcast(E4M3),
+                lhsT_scale=w1_scales[:, cols],
+                rhs=da_codes[e, h][:].bitcast(E5M2),
+                rhs_scale=da_scales[e, h][:],
+                start=(h == 0),
+                stop=(h == HALVES - 1),
+            )
+
+        slots = {}
+
+        def take(e):
+            slots[e] = ring.tile([P, C], F32, name="slots")
+            nc.scalar.copy(slots[e][:], dx[e][:])
+
+        def put_back(e):
+            nc.vector.tensor_copy(result[:].indirect(offsets[:, e * (C // 16) : (e + 1) * (C // 16)]), slots[e][:])
+
+        nc.vector.memset(one[:], 1.0)
+        nc.scalar.activation(one[:], one[:], SIGMOID)
+        nc.vector.memset(result[:], 0.0)
+
+        load_offs()
+        load_gate(0)
+        load_a(0, 0, 0, 2)
+        load_dy(0)
+        load_gate(1)
+        load_a(0, 0, 2, 4)
+        load_dy(1)
+        load_dy(3)
+        load_a(0, 1)
+        load_dy(2)
+        load_a(1, 0)
+        load_w1()
+        load_a(1, 1)
+        load_w2(1, 0)
+        load_w2(1, 1)
+        load_w2(0, 0)
+        load_w2(0, 1)
+
+        sigmoid(0, 0, 0, 2)
+        gather(0, 0)
+        gather(0, 1)
+        sigmoid(0, 0, 2, 4)
+        z1 = token(0, 0, "sig", "z1")
+        gather(1, 1)
+        gather(1, 0)
+        silu(0, 0, bias=z1)
+        gather(3, 1)
+        gather(3, 0)
+        silu(0, 1, bias=z1)
+        z2 = token(0, 1, "silu", "z2")
+        weigh(0, 0)
+        gather(2, 1)
+        sigmoid(0, 1, bias=z2)
+        gather(2, 0)
+        lay_g(1, "V")
+        sigmoid(1, 0, bias=z2)
+        weigh(0, 1)
+        sigmoid(1, 1, bias=z2)
+        z3 = token(1, 1, "sig", "z3")
+        quant_g(1)
+        lay_w1("V")
+        lay_g(0, "V")
+        lay_w2(1, 0, "V")
+        silu(1, 1, bias=z3)
+        lay_w2(1, 1, "V")
+        quant_w2(1, 0)
+        silu(1, 0, bias=z3)
+        lay_w2(0, 0, "V")
+        product(1, 0, 0)
+        product(1, 0, 2)
+        product(1, 0, 1)
+        product(1, 0, 3)
+        quant_w2(1, 1)
+        quant_w2(0, 0)
+        product(1, 1, 2)
+        evac(1, 0, 1)
+        product(1, 1, 1)
+        weigh(1, 1)
+        product(1, 1, 0)
+        evac(1, 1, 2)
+        product(1, 1, 3)
+        evac(1, 1, 1)
+        evac(1, 1, 0)
+        weigh(1, 0)
+        evac(1, 0, 2)
+        evac(1, 0, 3)
+        evac(1, 1, 3)
+        quant_g(0)
+        evac(1, 0, 0)
+        deriv(1, 1)
+        lay_w2(0, 1, "S")
+        product(0, 0, 3)
+        product(0, 0, 2)
+        product(0, 0, 1)
+        product(0, 0, 0)
+        deriv(1, 0)
+        evac(0, 0, 0)
+        evac(0, 0, 2)
+        evac(0, 0, 1)
+        quant_w2(0, 1)
+        evac(0, 0, 3)
+        quant_da(1, 0)
+        product(0, 1, 3)
+        product(0, 1, 2)
+        quant_da(1, 1)
+        evac(0, 1, 3)
+        product(0, 1, 0)
+        product(0, 1, 1)
+        deriv(0, 0)
+        evac(0, 1, 0)
+        evac(0, 1, 1)
+        evac(0, 1, 2)
+        quant_w1()
+        deriv(0, 1)
+        second(1, 0)
+        second(1, 1)
+        take(1)
+        quant_da(0, 0)
+        quant_da(0, 1)
+        second(0, 0)
+        put_back(1)
+        second(0, 1)
+        take(0)
+        put_back(0)
+        nc.sync.dma_start(out, result[:])

@@ -19,7 +19,9 @@ P = 128
 K, T, E, C, H, N = 128, 1536, 2, 512, 1024, 512
 S = E * C
 PACK = 4
-HALVES = H // 512
+PASS = P * PACK
+HALVES = H // PASS
+RUN = 4
 
 FLOPS = 2 * S * N * H + 2 * S * H * K
 BYTES = 4 * (N * T + H * S + E * N * H + E * H * K + S + K * T) + 2 * S
@@ -31,328 +33,231 @@ def tile_moe_bdx_mlp_silu_kernel(tc, dyT, a, w2, w1, gate, offs, out):
     a_rows = a.rearrange("(h p t) s -> p h t s", h=HALVES, t=PACK)
     w2_rows = w2.rearrange("e (p j) i -> p e j i", j=PACK)
     w1_rows = w1.rearrange("e (h p j) k -> p (e h) j k", h=HALVES, j=PACK)
+    pairs = [(e, h) for h in range(HALVES) for e in range(E)]
 
     with ExitStack() as ctx:
         lists = ctx.enter_context(tc.tile_pool(name="lists", bufs=1))
         keep = ctx.enter_context(tc.tile_pool(name="keep", bufs=1))
         ring = ctx.enter_context(tc.tile_pool(name="ring", bufs=2))
-        banks = ctx.enter_context(tc.psum_pool(name="banks", bufs=6))
-        sums = ctx.enter_context(tc.psum_pool(name="sums", bufs=2))
+        dh_banks = ctx.enter_context(tc.psum_pool(name="dh_banks", bufs=6))
+        dx_banks = ctx.enter_context(tc.psum_pool(name="dx_banks", bufs=2))
 
         offsets = lists.tile([P, S // 16], U16, name="offsets")
         gates = keep.tile([P, S], F32, name="gates")
         dy = [keep.tile([P, T], F32, name=f"dy{t}") for t in range(PACK)]
-        pre = {}
-        aux = {}
-        w2_raw = {}
-        for e in range(E):
-            for h in range(HALVES):
-                pre[e, h] = keep.tile([P, PACK, C], F32, name=f"pre{e}{h}")
-                aux[e, h] = keep.tile([P, PACK, C], F32, name=f"aux{e}{h}")
-                w2_raw[e, h] = keep.tile([P, PACK, 512], F32, name=f"w2raw{e}{h}")
-        w1_raw = keep.tile([P, E * HALVES, PACK, K], F32, name="w1raw")
+        v = [keep.tile([P, PACK, S], F32, name=f"v{h}") for h in range(HALVES)]
+        d = [keep.tile([P, PACK, S], F32, name=f"d{h}") for h in range(HALVES)]
+        w2_raw = {x: keep.tile([P, PACK, PASS], F32, name=f"w2_raw{x[0]}{x[1]}") for x in pairs}
+        w1_raw = keep.tile([P, E * HALVES, PACK, K], F32, name="w1_raw")
+        g_rows = keep.tile([P, PACK, S], F32, name="g_rows")
+
+        g_words = [keep.tile([P, C, PACK], BF16, name=f"g_words{e}", align_bytes=64) for e in range(E)]
+        g_codes = [keep.tile([P, C], U32, name=f"g_codes{e}", align_bytes=64) for e in range(E)]
+        g_scales = [keep.tile([P, C], U8, name=f"g_scales{e}", align_bytes=64) for e in range(E)]
+        w2_words = {x: keep.tile([P, PACK, P, PACK], BF16, name=f"w2_words{x[0]}{x[1]}", align_bytes=64) for x in pairs}
+        w2_codes = {x: keep.tile([P, PASS], U32, name=f"w2_codes{x[0]}{x[1]}", align_bytes=64) for x in pairs}
+        w2_scales = {x: keep.tile([P, PASS], U8, name=f"w2_scales{x[0]}{x[1]}", align_bytes=64) for x in pairs}
+        w1_words = keep.tile([P, E * HALVES, K, PACK], BF16, name="w1_words", align_bytes=64)
+        w1_codes = keep.tile([P, E * HALVES * K], U32, name="w1_codes", align_bytes=64)
+        w1_scales = keep.tile([P, E * HALVES * K], U8, name="w1_scales", align_bytes=64)
+        da_codes = {x: keep.tile([P, C], U32, name=f"da_codes{x[0]}{x[1]}", align_bytes=64) for x in pairs}
+        da_scales = {x: keep.tile([P, C], U8, name=f"da_scales{x[0]}{x[1]}", align_bytes=64) for x in pairs}
         result = keep.tile([P, T], F32, name="result")
-        one = keep.tile([P, 1], F32, name="one")
+        warm = keep.tile([P, 1], F32, name="warm")
+        zero = keep.tile([P, 1], F32, name="zero")
 
-        def load_offs():
-            nc.sync.dma_start(offsets[:], offs)
 
-        def load_gate(e):
-            nc.sync.dma_start(gates[:, e * C : (e + 1) * C], gate[0:P, e * C : (e + 1) * C])
-
-        def load_dy(t):
-            nc.sync.dma_start(dy[t][:], dy_rows[:, t, :])
-
-        def load_a(e, h, t0=0, t1=4):
-            nc.sync.dma_start(pre[e, h][:, t0:t1, :], a_rows[:, h, t0:t1, e * C : (e + 1) * C])
+        def load_a(h, t0, t1):
+            nc.sync.dma_start(v[h][:, t0:t1, :], a_rows[:, h, t0:t1, :])
 
         def load_w2(e, h):
-            nc.sync.dma_start(w2_raw[e, h][:], w2_rows[:, e, :, h * 512 : (h + 1) * 512])
+            nc.sync.dma_start(w2_raw[e, h][:], w2_rows[:, e, :, h * PASS : (h + 1) * PASS])
 
-        def load_w1():
-            nc.sync.dma_start(w1_raw[:], w1_rows)
+        def sigmoid(h, t):
+            nc.scalar.activation(d[h][:, t, :], v[h][:, t, :], SIGMOID, scale=(1.0, -1.0)[h])
 
-        first_of = {}
+        def silu(t):
+            nc.scalar.activation(v[1][:, t, :], v[1][:, t, :], SILU, bias=zero[:])
 
-        def sigmoid(e, h, t0=0, t1=4, bias=0.0):
-            first = first_of.setdefault((e, h), "sig") == "sig"
-            dst = aux[e, h] if first else pre[e, h]
-            nc.scalar.activation(dst[:, t0:t1, :], pre[e, h][:, t0:t1, :], SIGMOID, scale=-1.0, bias=bias)
+        def make_u(t):
+            nc.vector.scalar_tensor_tensor(v[0][:, t, :], d[0][:, t, :], -1.0, v[0][:, t, :], ADD, MULT)
 
-        def silu(e, h, t0=0, t1=4, bias=0.0):
-            first = first_of.setdefault((e, h), "silu") == "silu"
-            dst = aux[e, h] if first else pre[e, h]
-            nc.scalar.activation(dst[:, t0:t1, :], pre[e, h][:, t0:t1, :], SILU, bias=bias)
+        def make_z(h, t):
+            nc.vector.scalar_tensor_tensor(d[h][:, t, :], v[h][:, t, :], -1.0, d[h][:, t, :], ADD, MULT)
 
-        def token(e, h, func, name):
-            z = keep.tile([P, 1], F32, name=name)
-            src = aux[e, h] if first_of[e, h] == func else pre[e, h]
-            nc.scalar.activation(z[:], src[:, PACK - 1, C - 1 : C], COPY, scale=0.0)
-            return z[:]
+        last_step = [(-1.0, MULT), (1.0, ADD)]
 
-        def weigh(e, h):
-            y, s = (pre[e, h], aux[e, h]) if first_of[e, h] == "sig" else (aux[e, h], pre[e, h])
-            nc.vector.scalar_tensor_tensor(aux[e, h][:], y[:], -1.0, s[:], ADD, MULT)
+        def gather(t):
+            nc.vector.tensor_tensor(g_rows[:, t, :], dy[t][:].indirect(offsets[:]), gates[:], MULT)
 
-        g_rows = keep.tile([P, PACK, S], F32, name="grows")
-
-        def gather(t, e):
-            cols = slice(e * C, (e + 1) * C)
-            nc.vector.tensor_tensor(
-                g_rows[:, t, cols], dy[t][:].indirect(offsets[:, e * (C // 16) : (e + 1) * (C // 16)]), gates[:, cols], MULT
+        def interleave(copy, words, planes):
+            copy(
+                words.rearrange("p (c i) t -> p c t i", i=RUN),
+                planes.rearrange("p t (c i) -> p c t i", i=RUN),
             )
 
-        def copy_on(engine, dst, src):
-            if engine == "S":
-                nc.scalar.copy(dst, src)
-            elif engine == "V":
-                nc.vector.tensor_copy(dst, src)
-            else:
-                nc.gpsimd.tensor_scalar(dst, src, 1.0, 0.0, MULT, ADD)
+        def lay_g(e):
+            interleave(nc.vector.tensor_copy, g_words[e][:], g_rows[:, :, e * C : (e + 1) * C])
 
-        g_pairs = {}
-        g_codes = {}
-        g_scales = {}
-
-        def lay_g(e, engine):
-            g_pairs[e] = ring.tile([P, C, PACK], BF16, name="gpairs", align_bytes=64)
-            copy_on(
-                engine,
-                g_pairs[e][:].rearrange("p (c i) t -> p c t i", i=4),
-                g_rows[:, :, e * C : (e + 1) * C].rearrange("p t (c i) -> p c t i", i=4),
-            )
-
-        def quant_g(e):
-            g_codes[e] = keep.tile([P, C], U32, name=f"gcodes{e}", align_bytes=64)
-            g_scales[e] = keep.tile([P, C], U8, name=f"gscales{e}", align_bytes=64)
-            nc.vector.quantize_mx(out=g_codes[e][:].bitcast(E5M2), scales=g_scales[e][:], in_=g_pairs[e][:].rearrange("p c t -> p (c t)"))
-
-        w2_pairs = {}
-        w2_codes = {}
-        w2_scales = {}
-
-        def lay_w2(e, h, engine, part=None):
-            if (e, h) not in w2_pairs:
-                w2_pairs[e, h] = ring.tile([P, 4, 128, 4], BF16, name="w2pairs", align_bytes=64)
-            m = slice(0, 128) if part is None else slice(part * 64, part * 64 + 64)
-            src = w2_raw[e, h][:] if part is None else w2_raw[e, h][:, :, part * 256 : part * 256 + 256]
-            copy_on(
-                engine,
-                w2_pairs[e, h][:, :, m, :].rearrange("p t m j -> p m j t"),
-                src.rearrange("p j (m t) -> p m j t", t=4),
-            )
-
-        def quant_w2(e, h):
-            w2_codes[e, h] = keep.tile([P, 512], U32, name=f"w2codes{e}{h}", align_bytes=64)
-            w2_scales[e, h] = keep.tile([P, 512], U8, name=f"w2scales{e}{h}", align_bytes=64)
+        def quantize_g(e):
             nc.vector.quantize_mx(
-                out=w2_codes[e, h][:].bitcast(E4M3), scales=w2_scales[e, h][:], in_=w2_pairs[e, h][:].rearrange("p t m j -> p (t m j)")
+                out=g_codes[e][:].bitcast(E5M2), scales=g_scales[e][:], in_=g_words[e][:].rearrange("p c t -> p (c t)")
             )
 
-        w1_pairs = keep.tile([P, E * HALVES, K, PACK], BF16, name="w1pairs", align_bytes=64)
-        w1_codes = keep.tile([P, E * HALVES * K], U32, name="w1codes", align_bytes=64)
-        w1_scales = keep.tile([P, E * HALVES * K], U8, name="w1scales", align_bytes=64)
+        def lay_w2(e, h):
+            nc.scalar.copy(
+                w2_words[e, h][:].rearrange("p t m j -> p m j t"),
+                w2_raw[e, h][:].rearrange("p j (m t) -> p m j t", t=PACK),
+            )
 
-        def lay_w1(engine):
-            for u in range(E * HALVES):
-                copy_on(
-                    engine,
-                    w1_pairs[:, u].rearrange("p (c i) j -> p c j i", i=4),
-                    w1_raw[:, u].rearrange("p j (c i) -> p c j i", i=4),
+        def quantize_w2(e, h):
+            nc.vector.quantize_mx(
+                out=w2_codes[e, h][:].bitcast(E4M3),
+                scales=w2_scales[e, h][:],
+                in_=w2_words[e, h][:].rearrange("p t m j -> p (t m j)"),
+            )
+
+        def lay_w1():
+            for x in range(E * HALVES):
+                interleave(nc.scalar.copy, w1_words[:, x], w1_raw[:, x])
+
+        def quantize_w1():
+            nc.vector.quantize_mx(
+                out=w1_codes[:].bitcast(E4M3), scales=w1_scales[:], in_=w1_words[:].rearrange("p x k j -> p (x k j)")
+            )
+
+        da_planes = {}
+        da_words = {}
+
+        def make_da(e, h):
+            da_planes[e, h] = ring.tile([P, PACK, C], BF16, name="da_planes")
+            da_words[e, h] = ring.tile([P, C, PACK], BF16, name="da_words", align_bytes=64)
+            scalar, op = last_step[h]
+            for t in range(PACK):
+                dh = dh_banks.tile([P, C], F32, name="dh")
+                columns = slice(t * P, (t + 1) * P)
+                nc.tensor.matmul_mx(
+                    out=dh[:],
+                    lhsT=w2_codes[e, h][:, columns].bitcast(E4M3),
+                    lhsT_scale=w2_scales[e, h][:, columns],
+                    rhs=g_codes[e][:].bitcast(E5M2),
+                    rhs_scale=g_scales[e][:],
+                    start=True,
+                    stop=True,
+                )
+                nc.vector.scalar_tensor_tensor(
+                    da_planes[e, h][:, t, :], d[h][:, t, e * C : (e + 1) * C], scalar, dh[:], op, MULT
                 )
 
-        def quant_w1():
-            nc.vector.quantize_mx(out=w1_codes[:].bitcast(E4M3), scales=w1_scales[:], in_=w1_pairs[:].rearrange("p u k j -> p (u k j)"))
+        def lay_da(e, h, copy=nc.scalar.copy, c0=0, c1=C):
+            interleave(copy, da_words[e, h][:, c0:c1, :], da_planes[e, h][:, :, c0:c1])
 
-        bank = {}
-
-        def product(e, h, t):
-            bank[e, h, t] = banks.tile([P, C], F32, name="bank")
-            cols = slice(t * P, (t + 1) * P)
-            nc.tensor.matmul_mx(
-                out=bank[e, h, t][:],
-                lhsT=w2_codes[e, h][:, cols].bitcast(E4M3),
-                lhsT_scale=w2_scales[e, h][:, cols],
-                rhs=g_codes[e][:].bitcast(E5M2),
-                rhs_scale=g_scales[e][:],
-                start=True,
-                stop=True,
-            )
-
-        dh = {}
-        da_pairs = {}
-        da_planes = {}
-        da_codes = {}
-        da_scales = {}
-
-        def evac(e, h, t):
-            if (e, h) not in dh:
-                dh[e, h] = ring.tile([P, PACK, C], F32, name="dh")
-            nc.scalar.copy(dh[e, h][:, t, :], bank[e, h, t][:])
-
-        def deriv(e, h):
-            da_pairs[e, h] = ring.tile([P, C, PACK], BF16, name="dapairs", align_bytes=64)
-            nc.vector.scalar_tensor_tensor(
-                da_pairs[e, h][:],
-                aux[e, h][:].rearrange("p t c -> p c t"),
-                1.0,
-                dh[e, h][:].rearrange("p t c -> p c t"),
-                ADD,
-                MULT,
-            )
-
-        def deriv_bank(e, h, t):
-            if (e, h) not in da_planes:
-                da_planes[e, h] = ring.tile([P, PACK, C], BF16, name="daplanes")
-            nc.vector.scalar_tensor_tensor(da_planes[e, h][:, t, :], aux[e, h][:, t, :], 1.0, bank[e, h, t][:], ADD, MULT)
-
-        def lay_da(e, h, engine):
-            da_pairs[e, h] = ring.tile([P, C, PACK], BF16, name="dapairs", align_bytes=64)
-            copy_on(
-                engine,
-                da_pairs[e, h][:].rearrange("p (c i) t -> p c t i", i=4),
-                da_planes[e, h][:].rearrange("p t (c i) -> p c t i", i=4),
-            )
-
-        def quant_da(e, h):
-            da_codes[e, h] = ring.tile([P, C], U32, name="dacodes", align_bytes=64)
-            da_scales[e, h] = ring.tile([P, C], U8, name="dascales", align_bytes=64)
+        def quantize_da(e, h):
             nc.vector.quantize_mx(
-                out=da_codes[e, h][:].bitcast(E5M2), scales=da_scales[e, h][:], in_=da_pairs[e, h][:].rearrange("p c t -> p (c t)")
+                out=da_codes[e, h][:].bitcast(E5M2),
+                scales=da_scales[e, h][:],
+                in_=da_words[e, h][:].rearrange("p c t -> p (c t)"),
             )
 
-        dx = {}
+        dx = [dx_banks.tile([P, C], F32, name="dx") for e in range(E)]
 
-        def second(e, h):
-            if h == 0:
-                dx[e] = sums.tile([P, C], F32, name="dx")
-            u = e * HALVES + h
-            cols = slice(u * K, (u + 1) * K)
+        def add_to_dx(e, h):
+            columns = slice((e * HALVES + h) * K, (e * HALVES + h + 1) * K)
             nc.tensor.matmul_mx(
                 out=dx[e][:],
-                lhsT=w1_codes[:, cols].bitcast(E4M3),
-                lhsT_scale=w1_scales[:, cols],
+                lhsT=w1_codes[:, columns].bitcast(E4M3),
+                lhsT_scale=w1_scales[:, columns],
                 rhs=da_codes[e, h][:].bitcast(E5M2),
                 rhs_scale=da_scales[e, h][:],
                 start=(h == 0),
                 stop=(h == HALVES - 1),
             )
 
-        slots = {}
-
-        def take(e):
-            slots[e] = ring.tile([P, C], F32, name="slots")
-            nc.scalar.copy(slots[e][:], dx[e][:])
-
         def put_back(e):
-            nc.vector.tensor_copy(result[:].indirect(offsets[:, e * (C // 16) : (e + 1) * (C // 16)]), slots[e][:])
+            slots = ring.tile([P, C], F32, name="slots")
+            nc.scalar.copy(slots[:], dx[e][:])
+            nc.vector.tensor_copy(result[:].indirect(offsets[:, e * (C // 16) : (e + 1) * (C // 16)]), slots[:])
 
-        nc.vector.memset(one[:], 1.0)
-        nc.scalar.activation(one[:], one[:], SIGMOID)
+
+        nc.sync.dma_start(offsets[:], offs)
+        load_a(0, 0, 1)
+        load_a(0, 1, 2)
+        load_a(0, 2, 4)
+        load_a(1, 0, 2)
+        nc.sync.dma_start(gates[:], gate[0:P, :])
+        nc.sync.dma_start(dy[0][:], dy_rows[:, 0, :])
+        load_a(1, 2, 4)
+        for t in range(1, PACK):
+            nc.sync.dma_start(dy[t][:], dy_rows[:, t, :])
+        for e, h in pairs:
+            load_w2(e, h)
+        nc.sync.dma_start(w1_raw[:], w1_rows)
+
+
+        nc.vector.memset(warm[:], 1.0)
+        nc.scalar.activation(warm[:], warm[:], SIGMOID)
         nc.vector.memset(result[:], 0.0)
 
-        load_offs()
-        load_gate(0)
-        load_a(0, 0, 0, 2)
-        load_dy(0)
-        load_gate(1)
-        load_a(0, 0, 2, 4)
-        load_dy(1)
-        load_dy(3)
-        load_a(0, 1)
-        load_dy(2)
-        load_a(1, 0)
-        load_w1()
-        load_a(1, 1)
-        load_w2(1, 0)
-        load_w2(1, 1)
-        load_w2(0, 0)
-        load_w2(0, 1)
+        for t0 in (0, 2):
+            planes = range(t0, t0 + 2)
+            for t in planes:
+                sigmoid(0, t)
+            for t in planes:
+                make_u(t)
+            for t in planes:
+                make_z(0, t)
 
-        sigmoid(0, 0, 0, 2)
-        gather(0, 0)
-        gather(0, 1)
-        sigmoid(0, 0, 2, 4)
-        z1 = token(0, 0, "sig", "z1")
-        gather(1, 1)
-        gather(1, 0)
-        silu(0, 0, bias=z1)
-        gather(3, 1)
-        gather(3, 0)
-        silu(0, 1, bias=z1)
-        z2 = token(0, 1, "silu", "z2")
-        weigh(0, 0)
-        gather(2, 1)
-        sigmoid(0, 1, bias=z2)
-        gather(2, 0)
-        lay_g(1, "V")
-        sigmoid(1, 0, bias=z2)
-        weigh(0, 1)
-        sigmoid(1, 1, bias=z2)
-        z3 = token(1, 1, "sig", "z3")
-        quant_g(1)
-        lay_w1("V")
-        lay_g(0, "V")
-        lay_w2(1, 0, "V")
-        silu(1, 1, bias=z3)
-        lay_w2(1, 1, "V")
-        quant_w2(1, 0)
-        silu(1, 0, bias=z3)
-        lay_w2(0, 0, "V")
-        product(1, 0, 0)
-        product(1, 0, 2)
-        product(1, 0, 1)
-        product(1, 0, 3)
-        quant_w2(1, 1)
-        quant_w2(0, 0)
-        product(1, 1, 2)
-        evac(1, 0, 1)
-        product(1, 1, 1)
-        weigh(1, 1)
-        product(1, 1, 0)
-        evac(1, 1, 2)
-        product(1, 1, 3)
-        evac(1, 1, 1)
-        evac(1, 1, 0)
-        weigh(1, 0)
-        evac(1, 0, 2)
-        evac(1, 0, 3)
-        evac(1, 1, 3)
-        quant_g(0)
-        evac(1, 0, 0)
-        deriv(1, 1)
-        lay_w2(0, 1, "S")
-        product(0, 0, 3)
-        product(0, 0, 2)
-        product(0, 0, 1)
-        product(0, 0, 0)
-        deriv(1, 0)
-        evac(0, 0, 0)
-        evac(0, 0, 2)
-        evac(0, 0, 1)
-        quant_w2(0, 1)
-        evac(0, 0, 3)
-        quant_da(1, 0)
-        product(0, 1, 3)
-        product(0, 1, 2)
-        quant_da(1, 1)
-        evac(0, 1, 3)
-        product(0, 1, 0)
-        product(0, 1, 1)
-        deriv(0, 0)
-        evac(0, 1, 0)
-        evac(0, 1, 1)
-        evac(0, 1, 2)
-        quant_w1()
-        deriv(0, 1)
-        second(1, 0)
-        second(1, 1)
-        take(1)
-        quant_da(0, 0)
-        quant_da(0, 1)
-        second(0, 0)
-        put_back(1)
-        second(0, 1)
-        take(0)
+        sigmoid(1, 0)
+        sigmoid(1, 1)
+        gather(0)
+        gather(1)
+        sigmoid(1, 2)
+        sigmoid(1, 3)
+        nc.scalar.activation(zero[:], d[1][:, PACK - 1, S - 1 : S], COPY, scale=0.0)
+        silu(0)
+        silu(1)
+        gather(2)
+        gather(3)
+        silu(2)
+        lay_w2(0, 0)
+        make_z(1, 0)
+        lay_g(0)
+        quantize_w2(0, 0)
+        lay_w2(1, 0)
+        lay_g(1)
+        quantize_g(0)
+        quantize_g(1)
+        quantize_w2(1, 0)
+
+        make_da(0, 0)
+        lay_w2(0, 1)
+        quantize_w2(0, 1)
+        make_da(1, 0)
+        lay_w2(1, 1)
+        quantize_w2(1, 1)
+        make_z(1, 1)
+        lay_da(0, 0)
+        lay_da(1, 0)
+        quantize_da(0, 0)
+        quantize_da(1, 0)
+        silu(3)
+        lay_w1()
+        make_z(1, 2)
+        make_z(1, 3)
+
+        make_da(0, 1)
+        make_da(1, 1)
+        quantize_w1()
+        add_to_dx(0, 0)
+        add_to_dx(1, 0)
+        lay_da(0, 1)
+        quantize_da(0, 1)
+        add_to_dx(0, 1)
+        lay_da(1, 1, nc.scalar.copy, 0, C // 2)
+        lay_da(1, 1, nc.vector.tensor_copy, C // 2, C)
+        quantize_da(1, 1)
+        add_to_dx(1, 1)
         put_back(0)
+        put_back(1)
+
         nc.sync.dma_start(out, result[:])

from contextlib import ExitStack

import concourse.mybir as mybir

F32 = mybir.dt.float32
BF16 = mybir.dt.bfloat16
U32 = mybir.dt.uint32
U16 = mybir.dt.uint16
U8 = mybir.dt.uint8
E4M3 = mybir.dt.float8_e4m3fn_x4
E5M2 = mybir.dt.float8_e5m2_x4
ADD = mybir.AluOpType.add
MULT = mybir.AluOpType.mult
COPY = mybir.ActivationFunctionType.Copy
SIGMOID = mybir.ActivationFunctionType.Sigmoid
SILU = mybir.ActivationFunctionType.Silu

P = 128
K, T, E, C, H, N = 128, 1536, 2, 512, 1024, 512
S = E * C
PACK = 4
PASS = P * PACK
HALVES = H // PASS
RUN = 4

FLOPS = 2 * S * N * H + 2 * S * H * K
BYTES = 4 * (N * T + H * S + E * N * H + E * H * K + S + K * T) + 2 * S


def tile_moe_bdx_mlp_silu_kernel(tc, dyT, a, w2, w1, gate, offs, out):
    nc = tc.nc
    dy_rows = dyT.rearrange("(p t) s -> p t s", t=PACK)
    a_rows = a.rearrange("(h p t) s -> p h t s", h=HALVES, t=PACK)
    w2_rows = w2.rearrange("e (p j) i -> p e j i", j=PACK)
    w1_rows = w1.rearrange("e (h p j) k -> p (e h) j k", h=HALVES, j=PACK)
    pairs = [(e, h) for h in range(HALVES) for e in range(E)]

    with ExitStack() as ctx:
        lists = ctx.enter_context(tc.tile_pool(name="lists", bufs=1))
        keep = ctx.enter_context(tc.tile_pool(name="keep", bufs=1))
        ring = ctx.enter_context(tc.tile_pool(name="ring", bufs=2))
        dh_banks = ctx.enter_context(tc.psum_pool(name="dh_banks", bufs=6))
        dx_banks = ctx.enter_context(tc.psum_pool(name="dx_banks", bufs=2))

        offsets = lists.tile([P, S // 16], U16, name="offsets")
        gates = keep.tile([P, S], F32, name="gates")
        dy = [keep.tile([P, T], F32, name=f"dy{t}") for t in range(PACK)]
        v = [keep.tile([P, PACK, S], F32, name=f"v{h}") for h in range(HALVES)]
        d = [keep.tile([P, PACK, S], F32, name=f"d{h}") for h in range(HALVES)]
        w2_raw = {x: keep.tile([P, PACK, PASS], F32, name=f"w2_raw{x[0]}{x[1]}") for x in pairs}
        w1_raw = keep.tile([P, E * HALVES, PACK, K], F32, name="w1_raw")
        g_rows = keep.tile([P, PACK, S], F32, name="g_rows")

        g_words = [keep.tile([P, C, PACK], BF16, name=f"g_words{e}", align_bytes=64) for e in range(E)]
        g_codes = [keep.tile([P, C], U32, name=f"g_codes{e}", align_bytes=64) for e in range(E)]
        g_scales = [keep.tile([P, C], U8, name=f"g_scales{e}", align_bytes=64) for e in range(E)]
        w2_words = {x: keep.tile([P, PACK, P, PACK], BF16, name=f"w2_words{x[0]}{x[1]}", align_bytes=64) for x in pairs}
        w2_codes = {x: keep.tile([P, PASS], U32, name=f"w2_codes{x[0]}{x[1]}", align_bytes=64) for x in pairs}
        w2_scales = {x: keep.tile([P, PASS], U8, name=f"w2_scales{x[0]}{x[1]}", align_bytes=64) for x in pairs}
        w1_words = keep.tile([P, E * HALVES, K, PACK], BF16, name="w1_words", align_bytes=64)
        w1_codes = keep.tile([P, E * HALVES * K], U32, name="w1_codes", align_bytes=64)
        w1_scales = keep.tile([P, E * HALVES * K], U8, name="w1_scales", align_bytes=64)
        da_codes = {x: keep.tile([P, C], U32, name=f"da_codes{x[0]}{x[1]}", align_bytes=64) for x in pairs}
        da_scales = {x: keep.tile([P, C], U8, name=f"da_scales{x[0]}{x[1]}", align_bytes=64) for x in pairs}
        result = keep.tile([P, T], F32, name="result")
        warm = keep.tile([P, 1], F32, name="warm")
        zero = keep.tile([P, 1], F32, name="zero")


        def load_a(h, t0, t1):
            nc.sync.dma_start(v[h][:, t0:t1, :], a_rows[:, h, t0:t1, :])

        def load_w2(e, h):
            nc.sync.dma_start(w2_raw[e, h][:], w2_rows[:, e, :, h * PASS : (h + 1) * PASS])

        def sigmoid(h, t):
            nc.scalar.activation(d[h][:, t, :], v[h][:, t, :], SIGMOID, scale=(1.0, -1.0)[h])

        def silu(t):
            nc.scalar.activation(v[1][:, t, :], v[1][:, t, :], SILU, bias=zero[:])

        def make_u(t):
            nc.vector.scalar_tensor_tensor(v[0][:, t, :], d[0][:, t, :], -1.0, v[0][:, t, :], ADD, MULT)

        def make_z(h, t):
            nc.vector.scalar_tensor_tensor(d[h][:, t, :], v[h][:, t, :], -1.0, d[h][:, t, :], ADD, MULT)

        last_step = [(-1.0, MULT), (1.0, ADD)]

        def gather(t):
            nc.vector.tensor_tensor(g_rows[:, t, :], dy[t][:].indirect(offsets[:]), gates[:], MULT)

        def interleave(copy, words, planes):
            copy(
                words.rearrange("p (c i) t -> p c t i", i=RUN),
                planes.rearrange("p t (c i) -> p c t i", i=RUN),
            )

        def lay_g(e):
            interleave(nc.vector.tensor_copy, g_words[e][:], g_rows[:, :, e * C : (e + 1) * C])

        def quantize_g(e):
            nc.vector.quantize_mx(
                out=g_codes[e][:].bitcast(E5M2), scales=g_scales[e][:], in_=g_words[e][:].rearrange("p c t -> p (c t)")
            )

        def lay_w2(e, h):
            nc.scalar.copy(
                w2_words[e, h][:].rearrange("p t m j -> p m j t"),
                w2_raw[e, h][:].rearrange("p j (m t) -> p m j t", t=PACK),
            )

        def quantize_w2(e, h):
            nc.vector.quantize_mx(
                out=w2_codes[e, h][:].bitcast(E4M3),
                scales=w2_scales[e, h][:],
                in_=w2_words[e, h][:].rearrange("p t m j -> p (t m j)"),
            )

        def lay_w1():
            for x in range(E * HALVES):
                interleave(nc.scalar.copy, w1_words[:, x], w1_raw[:, x])

        def quantize_w1():
            nc.vector.quantize_mx(
                out=w1_codes[:].bitcast(E4M3), scales=w1_scales[:], in_=w1_words[:].rearrange("p x k j -> p (x k j)")
            )

        da_planes = {}
        da_words = {}

        def make_da(e, h):
            da_planes[e, h] = ring.tile([P, PACK, C], BF16, name="da_planes")
            da_words[e, h] = ring.tile([P, C, PACK], BF16, name="da_words", align_bytes=64)
            scalar, op = last_step[h]
            for t in range(PACK):
                dh = dh_banks.tile([P, C], F32, name="dh")
                columns = slice(t * P, (t + 1) * P)
                nc.tensor.matmul_mx(
                    out=dh[:],
                    lhsT=w2_codes[e, h][:, columns].bitcast(E4M3),
                    lhsT_scale=w2_scales[e, h][:, columns],
                    rhs=g_codes[e][:].bitcast(E5M2),
                    rhs_scale=g_scales[e][:],
                    start=True,
                    stop=True,
                )
                nc.vector.scalar_tensor_tensor(
                    da_planes[e, h][:, t, :], d[h][:, t, e * C : (e + 1) * C], scalar, dh[:], op, MULT
                )

        def lay_da(e, h, copy=nc.scalar.copy, c0=0, c1=C):
            interleave(copy, da_words[e, h][:, c0:c1, :], da_planes[e, h][:, :, c0:c1])

        def quantize_da(e, h):
            nc.vector.quantize_mx(
                out=da_codes[e, h][:].bitcast(E5M2),
                scales=da_scales[e, h][:],
                in_=da_words[e, h][:].rearrange("p c t -> p (c t)"),
            )

        dx = [dx_banks.tile([P, C], F32, name="dx") for e in range(E)]

        def add_to_dx(e, h):
            columns = slice((e * HALVES + h) * K, (e * HALVES + h + 1) * K)
            nc.tensor.matmul_mx(
                out=dx[e][:],
                lhsT=w1_codes[:, columns].bitcast(E4M3),
                lhsT_scale=w1_scales[:, columns],
                rhs=da_codes[e, h][:].bitcast(E5M2),
                rhs_scale=da_scales[e, h][:],
                start=(h == 0),
                stop=(h == HALVES - 1),
            )

        def put_back(e):
            slots = ring.tile([P, C], F32, name="slots")
            nc.scalar.copy(slots[:], dx[e][:])
            nc.vector.tensor_copy(result[:].indirect(offsets[:, e * (C // 16) : (e + 1) * (C // 16)]), slots[:])


        nc.sync.dma_start(offsets[:], offs)
        load_a(0, 0, 1)
        load_a(0, 1, 2)
        load_a(0, 2, 4)
        load_a(1, 0, 2)
        nc.sync.dma_start(gates[:], gate[0:P, :])
        nc.sync.dma_start(dy[0][:], dy_rows[:, 0, :])
        load_a(1, 2, 4)
        for t in range(1, PACK):
            nc.sync.dma_start(dy[t][:], dy_rows[:, t, :])
        for e, h in pairs:
            load_w2(e, h)
        nc.sync.dma_start(w1_raw[:], w1_rows)


        nc.vector.memset(warm[:], 1.0)
        nc.scalar.activation(warm[:], warm[:], SIGMOID)
        nc.vector.memset(result[:], 0.0)

        for t0 in (0, 2):
            planes = range(t0, t0 + 2)
            for t in planes:
                sigmoid(0, t)
            for t in planes:
                make_u(t)
            for t in planes:
                make_z(0, t)

        sigmoid(1, 0)
        sigmoid(1, 1)
        gather(0)
        gather(1)
        sigmoid(1, 2)
        sigmoid(1, 3)
        nc.scalar.activation(zero[:], d[1][:, PACK - 1, S - 1 : S], COPY, scale=0.0)
        silu(0)
        silu(1)
        gather(2)
        gather(3)
        silu(2)
        lay_w2(0, 0)
        make_z(1, 0)
        lay_g(0)
        quantize_w2(0, 0)
        lay_w2(1, 0)
        lay_g(1)
        quantize_g(0)
        quantize_g(1)
        quantize_w2(1, 0)

        make_da(0, 0)
        lay_w2(0, 1)
        quantize_w2(0, 1)
        make_da(1, 0)
        lay_w2(1, 1)
        quantize_w2(1, 1)
        make_z(1, 1)
        lay_da(0, 0)
        lay_da(1, 0)
        quantize_da(0, 0)
        quantize_da(1, 0)
        silu(3)
        lay_w1()
        make_z(1, 2)
        make_z(1, 3)

        make_da(0, 1)
        make_da(1, 1)
        quantize_w1()
        add_to_dx(0, 0)
        add_to_dx(1, 0)
        lay_da(0, 1)
        quantize_da(0, 1)
        add_to_dx(0, 1)
        lay_da(1, 1, nc.scalar.copy, 0, C // 2)
        lay_da(1, 1, nc.vector.tensor_copy, C // 2, C)
        quantize_da(1, 1)
        add_to_dx(1, 1)
        put_back(0)
        put_back(1)

        nc.sync.dma_start(out, result[:])
